import numpy as np
import ml_dtypes


def mxq(x, axis, fmt="e4m3"):
    dtype, down = {"e4m3": (ml_dtypes.float8_e4m3fn, 7), "e5m2": (ml_dtypes.float8_e5m2, 14)}[fmt]
    v = np.moveaxis(np.asarray(x, np.float32).astype(ml_dtypes.bfloat16).astype(np.float64), axis, -1)
    blocks = v.reshape(v.shape[:-1] + (-1, 32))
    amax = np.abs(blocks).max(-1, keepdims=True)
    byte = np.maximum(np.where(amax > 0, np.frexp(amax)[1] - 1 + 127, 0) - down, 1)
    scale = np.exp2(byte - 127.0)
    codes = (blocks / scale).astype(np.float32).astype(dtype).astype(np.float64)
    return np.moveaxis((codes * scale).reshape(v.shape), -1, axis)


WIDE = False


def mx_kscale(k):
    if not WIDE:
        return np.ones(k)
    levels = np.array([10, -10, 5, -5, 0])
    if k % 512:
        return np.exp2(np.random.permutation(np.resize(levels, k // 32))).repeat(32)
    a = np.empty((k // 512, 16))
    for p in range(k // 512):
        a[p, :8] = np.random.permutation(np.resize(levels, 8))
        for g in range(8):
            far = levels[np.abs(levels - a[p, g]) >= 10]
            a[p, g + 8] = far[np.random.randint(len(far))]
    return np.exp2(a.ravel()).repeat(32)


def f64(x):
    return np.asarray(x).astype(np.float64)


def striped(idx):
    return np.tile(np.asarray(idx).reshape(-1, 16).T, (8, 1)).astype(np.uint16)


def unstriped(offs):
    return offs[:16].T.reshape(-1).astype(np.int64)


E2M1 = np.array([0.0, 0.5, 1.0, 1.5, 2.0, 3.0, 4.0, 6.0, -0.0, -0.5, -1.0, -1.5, -2.0, -3.0, -4.0, -6.0])


def pack_weight(w, fmt):
    k, n = w.shape
    w = f64(np.asarray(w, np.float32).astype(ml_dtypes.bfloat16)).reshape(k // 32, 32, n)
    amax = np.abs(w).max(1)
    if fmt == "e4m3":
        byte = np.frexp(amax)[1] - 1 + 127 - 7
    else:
        mant, ex = np.frexp(amax / 6.0)
        byte = np.where(mant > 0.5, ex, ex - 1) + 127
    byte = np.clip(np.where(amax > 0, byte, 1), 1, 254)
    scaled = (w * np.exp2(127.0 - byte)[:, None, :]).reshape(k, n).astype(np.float32)
    by_word = np.ascontiguousarray(scaled.reshape(k // 512, 128, 4, n).transpose(0, 1, 3, 2))
    if fmt == "e4m3":
        words = by_word.astype(ml_dtypes.float8_e4m3fn).view(np.uint8)
    else:
        c = by_word.astype(ml_dtypes.float4_e2m1fn).view(np.uint8) & 0xF
        words = (c[..., 0::2] | (c[..., 1::2] << 4)).reshape(k // 512, 128, 2 * n)
    return np.ascontiguousarray(words), np.ascontiguousarray(byte.astype(np.uint8).reshape(k // 512, 16, n))


def unpack_weight(words, scales, fmt):
    g, _, n = scales.shape
    words = np.ascontiguousarray(words).reshape(g, 128, n, -1)
    if fmt == "e4m3":
        vals = words.view(ml_dtypes.float8_e4m3fn).astype(np.float64)
    else:
        nib = np.empty((g, 128, n, 4), np.uint8)
        nib[..., 0::2] = words & 0xF
        nib[..., 1::2] = words >> 4
        vals = E2M1[nib]
    vals = vals * np.repeat(np.exp2(scales.astype(np.float64) - 127.0), 8, axis=1)[..., None]
    return vals.transpose(0, 1, 3, 2).reshape(g * 512, n)


def sigmoid(v):
    return 1.0 / (1.0 + np.exp(-v))


def bf(x):
    return np.asarray(x, np.float32).astype(ml_dtypes.bfloat16)


def planes(Y):
    r, m = Y.shape
    b = f64(bf(Y)).reshape(r // 32, 32, m)
    amax = np.abs(b).max(1)
    byte = np.clip(np.where(amax > 0, np.frexp(amax)[1] - 1 + 127 - 7, 1), 1, 254)
    codes = (b * np.exp2(127.0 - byte)[:, None, :]).reshape(r, m).astype(np.float32).astype(ml_dtypes.float8_e4m3fn).view(np.uint8)
    words = codes.reshape(r // 512, 128, 4, m).transpose(0, 1, 3, 2)
    return np.ascontiguousarray(words), np.ascontiguousarray(byte.astype(np.uint8).reshape(r // 512, 16, m))


K, T, J, N = 1024, 1024, 512, 512


def setup_inputs():
    n = np.random.standard_normal
    idx = np.random.permutation(T)[:J]
    fk = mx_kscale(K)
    wap = pack_weight(n((K, N)) * 1 / np.sqrt(K) * fk[:, None], "e2m1")
    wgp = pack_weight(n((K, N)) * 1 / np.sqrt(K) * fk[:, None], "e4m3")
    return {
        "xt": (n((K, T)) / fk[:, None]).astype(np.float32),
        "wa_words": wap[0],
        "wa_scales": wap[1],
        "wg_words": wgp[0],
        "wg_scales": wgp[1],
        "old": (1.0 * n((N, T))).astype(np.float32),
        "offs": striped(idx),
    }


def reference(xt, wa_words, wa_scales, wg_words, wg_scales, old, offs):
    idx = unstriped(offs)
    wau = unpack_weight(wa_words, wa_scales, "e2m1")
    wgu = unpack_weight(wg_words, wg_scales, "e4m3")
    xtidxq = mxq(f64(xt)[:, idx], 0, "e4m3")
    a = wau.T @ xtidxq
    g = wgu.T @ xtidxq
    d = f64(old)[:, idx] * sigmoid(g) - f64(old)[:, idx] + a
    dp = np.zeros((N, T))
    dp[:, idx] = d
    y = f64(old) + dp
    words, scales = planes(y)
    return y, words, scales

@@ -1,0 +1,216 @@
+from contextlib import ExitStack
+
+import concourse.mybir as mybir
+
+K, T, J, N = 1024, 1024, 512, 512
+FLOPS = 2 * 2 * K * N * J
+
+F32 = mybir.dt.float32
+BF16 = mybir.dt.bfloat16
+I32 = mybir.dt.int32
+U32 = mybir.dt.uint32
+U16 = mybir.dt.uint16
+U8 = mybir.dt.uint8
+FP8X4 = mybir.dt.float8_e4m3fn_x4
+FP4X4 = mybir.dt.float4_e2m1fn_x4
+ACT = mybir.ActivationFunctionType
+ALU = mybir.AluOpType
+
+P = 128
+PACK = 4
+PASSES = K // (P * PACK)
+HALF = T // 2
+WG_ROW = 4
+TAIL = 256
+
+
+def tile_moe_expert_page_fades_where_written_pl_kernel(
+    tc, xt, wa_words, wa_scales, wg_words, wg_scales, old, offs, out_0, out_1, out_2
+):
+    nc = tc.nc
+    with ExitStack() as ctx:
+        keep = ctx.enter_context(tc.tile_pool(name="keep", bufs=1))
+        psum = ctx.enter_context(tc.psum_pool(name="psum", bufs=1))
+
+        offsets = keep.tile([P, J // 16], U16, name="offsets")
+        nc.sync.dma_start(offsets[:], offs)
+
+        scale_raw = keep.tile([P, PASSES * N], U8, name="scale_raw")
+        nc.vector.memset(scale_raw[:].bitcast(I32), 0)
+        faded = [keep.tile([P, T], F32, name=f"faded{t}") for t in range(PACK)]
+        for t in range(PACK):
+            nc.vector.memset(faded[t][:], 0.0)
+
+        x_rows = xt.rearrange("(a p u e) c -> a u p e c", a=PASSES, p=P, u=2, e=2)
+        x_raw = {}
+
+        def load_x(a, u, width):
+            for c0 in range(0, T, width):
+                raw = keep.tile([P, 2, width], F32, name=f"x_raw{a}{u}{c0}")
+                nc.sync.dma_start(raw[:], x_rows[a, u, :, :, c0 : c0 + width])
+                x_raw[a, u, c0] = raw
+
+        def load_scales(scales, row0):
+            rows = scales.bitcast(I32).rearrange("a (q r) n -> r q a n", r=4)
+            for r in range(4):
+                dst = scale_raw[row0 + r : P : 32, :].bitcast(I32)
+                nc.sync.dma_start(dst.rearrange("q (a n) -> q a n", a=PASSES), rows[r])
+
+        load_x(0, 0, T)
+        load_x(0, 1, T)
+        wg_raw = keep.tile([P, PASSES, N], I32, name="wg_raw")
+        nc.sync.dma_start(wg_raw[:], wg_words.rearrange("a p n r -> p a (n r)").bitcast(I32))
+        wa_raw = keep.tile([P, PASSES * N // 2], I32, name="wa_raw")
+        nc.sync.dma_start(
+            wa_raw[:].rearrange("p (a n) -> p a n", a=PASSES),
+            wa_words.rearrange("a p b -> p a b").bitcast(I32),
+        )
+        load_scales(wa_scales, 0)
+        load_x(1, 0, HALF)
+        load_scales(wg_scales, WG_ROW)
+        load_x(1, 1, HALF)
+        old_rows = old.rearrange("(p t) c -> t p c", t=PACK)
+        page = [keep.tile([P, T], F32, name=f"page{t}") for t in range(PACK)]
+        for t in range(PACK):
+            nc.sync.dma_start(page[t][:], old_rows[t])
+
+        x_in = [keep.tile([P, 2 * J], U32, name=f"x_in{a}", align_bytes=64) for a in range(PASSES)]
+        x_codes = [keep.tile([P, J], U32, name=f"x_codes{a}", align_bytes=64) for a in range(PASSES)]
+        x_scales = [keep.tile([P, J], U8, name=f"x_scales{a}", align_bytes=64) for a in range(PASSES)]
+
+        def cast_pairs(engine, pairs, a, u, h, c0, c1):
+            dst = pairs[:, h + c0 : h + c1].bitcast(BF16).rearrange("p (c e) -> p c e", e=2)
+            src = x_raw[a, u, h][:, :, c0:c1].rearrange("p e c -> p c e")
+            if engine == "vector":
+                nc.vector.tensor_copy(dst, src)
+            else:
+                nc.scalar.activation(dst, src, ACT.Copy)
+
+        def gather_x(a, u):
+            pairs = keep.tile([P, T], U32, name=f"pairs{a}{u}")
+            if a == 0:
+                cast_pairs("scalar", pairs, a, u, 0, 0, HALF)
+                cast_pairs("vector", pairs, a, u, 0, HALF, T)
+            elif u == 0:
+                cast_pairs("scalar", pairs, a, u, 0, 0, HALF)
+                cast_pairs("scalar", pairs, a, u, HALF, 0, HALF)
+            else:
+                cast_pairs("scalar", pairs, a, u, 0, 0, HALF)
+                cast_pairs("scalar", pairs, a, u, HALF, 0, 192)
+                cast_pairs("vector", pairs, a, u, HALF, 192, HALF)
+            dst = x_in[a][:].rearrange("p (j u) -> p j u", u=2)[:, :, u]
+            nc.vector.tensor_copy(dst, pairs[:].indirect(offsets[:]))
+
+        def quantize_x(a):
+            nc.vector.quantize_mx(
+                out=x_codes[a][:].bitcast(FP8X4), scales=x_scales[a][:], in_=x_in[a][:].bitcast(BF16)
+            )
+
+        gather_x(0, 0)
+        gather_x(0, 1)
+        quantize_x(0)
+
+        wg = keep.tile([P, PASSES * N], I32, name="wg", align_bytes=64)
+        nc.vector.tensor_copy(
+            wg[:].rearrange("p (a t m) -> p a m t", a=PASSES, t=PACK),
+            wg_raw[:].rearrange("p a (m t) -> p a m t", t=PACK),
+        )
+        wa = keep.tile([P, PASSES * N * 2], U8, name="wa", align_bytes=64)
+        nc.vector.tensor_copy(
+            wa[:].bitcast(U16).rearrange("p (a t m) -> p a m t", a=PASSES, t=PACK),
+            wa_raw[:].bitcast(U16).rearrange("p (a m t) -> p a m t", a=PASSES, t=PACK),
+        )
+        w_scales = keep.tile([P, PASSES * N], U8, name="w_scales", align_bytes=64)
+        nc.vector.tensor_copy(
+            w_scales[:].rearrange("p (a t m) -> p a m t", a=PASSES, t=PACK),
+            scale_raw[:].rearrange("p (a m t) -> p a m t", a=PASSES, t=PACK),
+        )
+
+        gather_x(1, 0)
+        gather_x(1, 1)
+        quantize_x(1)
+
+        g_sum = [psum.tile([P, J], F32, name=f"g_sum{t}") for t in range(PACK)]
+        a_sum = [psum.tile([P, J], F32, name=f"a_sum{t}") for t in range(PACK)]
+        for a in range(PASSES):
+            for t in range(PACK):
+                c0 = a * N + t * P
+                nc.tensor.matmul_mx(
+                    out=g_sum[t][:],
+                    lhsT=wg[:, c0 : c0 + P].bitcast(FP8X4),
+                    lhsT_scale=w_scales[WG_ROW:P, c0 : c0 + P],
+                    rhs=x_codes[a][:].bitcast(FP8X4),
+                    rhs_scale=x_scales[a][:],
+                    start=(a == 0),
+                    stop=(a == PASSES - 1),
+                )
+                nc.tensor.matmul_mx(
+                    out=a_sum[t][:],
+                    lhsT=wa[:, 2 * c0 : 2 * (c0 + P)].bitcast(FP4X4),
+                    lhsT_scale=w_scales[:, c0 : c0 + P],
+                    rhs=x_codes[a][:].bitcast(FP8X4),
+                    rhs_scale=x_scales[a][:],
+                    start=(a == 0),
+                    stop=(a == PASSES - 1),
+                )
+
+        y = [keep.tile([P, 2, T], F32, name=f"y{u}") for u in range(2)]
+        y_in = keep.tile([P, T * PACK], BF16, name="y_in", align_bytes=64)
+        y_codes = keep.tile([P, T], U32, name="y_codes", align_bytes=64)
+        y_scales = keep.tile([P, T], U8, name="y_scales", align_bytes=64)
+        out_rows = out_0.rearrange("(p t) c -> t p c", t=PACK)
+        out_words = out_1[0].rearrange("p c r -> p (c r)").bitcast(I32)
+
+        picked = keep.tile([P, J], F32, name="picked")
+        nc.vector.tensor_copy(picked[:], page[0][:].indirect(offsets[:]))
+
+        lost, minus_a = [], []
+        for t in range(PACK):
+            fade = keep.tile([P, J], F32, name=f"fade{t}")
+            nc.scalar.activation(fade[:], g_sum[t][:], ACT.Sigmoid, scale=-1.0)
+            neg = keep.tile([P, J], F32, name=f"minus_a{t}")
+            nc.scalar.activation(neg[:], a_sum[t][:], ACT.Copy, scale=-1.0)
+            minus_a.append(neg)
+            prod = keep.tile([P, J], F32, name=f"lost{t}")
+            if t == 0:
+                nc.vector.tensor_tensor(prod[:], picked[:], fade[:], ALU.mult)
+            else:
+                nc.vector.tensor_tensor(prod[:], page[t][:].indirect(offsets[:]), fade[:], ALU.mult)
+            lost.append(prod)
+
+        def round_pair(engine, u, c0, c1):
+            dst = y_in[:].rearrange("p (c r) -> p c r", r=PACK)[:, c0:c1, 2 * u : 2 * u + 2]
+            src = y[u][:, :, c0:c1].rearrange("p e c -> p c e")
+            if engine == "vector":
+                nc.vector.tensor_copy(dst, src)
+            else:
+                nc.scalar.copy(dst, src)
+
+        for t in range(PACK):
+            nc.vector.tensor_tensor(faded[t][:].indirect(offsets[:]), lost[t][:], minus_a[t][:], ALU.add)
+            if t < PACK - 1:
+                nc.vector.tensor_tensor(y[t // 2][:, t % 2, :], page[t][:], faded[t][:], ALU.subtract)
+                nc.sync.dma_start(out_rows[t], y[t // 2][:, t % 2, :])
+            if t == 1:
+                round_pair("scalar", 0, 0, T)
+
+        last = PACK - 1
+        for c0 in range(0, T, TAIL):
+            cols = slice(c0, c0 + TAIL)
+            nc.vector.tensor_tensor(y[1][:, 1, cols], page[last][:, cols], faded[last][:, cols], ALU.subtract)
+        for c0 in range(0, T, HALF):
+            nc.sync.dma_start(out_rows[last][:, c0 : c0 + HALF], y[1][:, 1, c0 : c0 + HALF])
+        for c0 in range(0, T, TAIL):
+            round_pair("vector" if c0 >= HALF else "scalar", 1, c0, c0 + TAIL)
+        for c0 in (HALF, 0, HALF + TAIL, TAIL):
+            cols = slice(c0, c0 + TAIL)
+            nc.vector.quantize_mx(
+                out=y_codes[:, cols].bitcast(FP8X4),
+                scales=y_scales[:, cols],
+                in_=y_in[:, PACK * c0 : PACK * (c0 + TAIL)],
+            )
+            nc.sync.dma_start(out_words[:, cols], y_codes[:, cols].bitcast(I32))
+        scale_rows = out_2[0].bitcast(I32).rearrange("(q r) c -> r q c", r=4)
+        for r in range(4):
+            queue = nc.scalar if r % 2 else nc.sync
+            queue.dma_start(scale_rows[r], y_scales[r:P:32, :].bitcast(I32))

@@ -1,6 +1,7 @@
 from contextlib import ExitStack
 
 import concourse.mybir as mybir
+from concourse.masks import make_identity
 
 K, T, J, N = 1024, 1024, 512, 512
 FLOPS = 2 * 2 * K * N * J
@@ -33,42 +34,46 @@ def tile_moe_expert_page_fades_where_written_pl_kernel(
         psum = ctx.enter_context(tc.psum_pool(name="psum", bufs=1))
 
         offsets = keep.tile([P, J // 16], U16, name="offsets")
-        nc.sync.dma_start(offsets[:], offs)
 
         scale_raw = keep.tile([P, PASSES * N], U8, name="scale_raw")
+        scale_in = keep.tile([P, PASSES * N // 4], I32, name="scale_in")
         nc.vector.memset(scale_raw[:].bitcast(I32), 0)
         faded = [keep.tile([P, T], F32, name=f"faded{t}") for t in range(PACK)]
         for t in range(PACK):
             nc.vector.memset(faded[t][:], 0.0)
 
+        identity = keep.tile([P, P], F32, name="identity")
+        make_identity(nc, identity[:])
+
         x_rows = xt.rearrange("(a p u e) c -> a u p e c", a=PASSES, p=P, u=2, e=2)
         x_raw = {}
 
-        def load_x(a, u, width):
-            for c0 in range(0, T, width):
-                raw = keep.tile([P, 2, width], F32, name=f"x_raw{a}{u}{c0}")
-                nc.sync.dma_start(raw[:], x_rows[a, u, :, :, c0 : c0 + width])
-                x_raw[a, u, c0] = raw
+        def load_x(a, u):
+            for h in range(2):
+                raw = keep.tile([P, 2, HALF], F32, name=f"x_raw{a}{u}{h}")
+                nc.sync.dma_start(raw[:], x_rows[a, u, :, :, h * HALF : (h + 1) * HALF])
+                x_raw[a, u, h] = raw
 
         def load_scales(scales, row0):
             rows = scales.bitcast(I32).rearrange("a (q r) n -> r q a n", r=4)
             for r in range(4):
-                dst = scale_raw[row0 + r : P : 32, :].bitcast(I32)
-                nc.sync.dma_start(dst.rearrange("q (a n) -> q a n", a=PASSES), rows[r])
+                dst = scale_in[row0 + r : P : 32, :]
+                nc.scalar.dma_start(dst.rearrange("q (a n) -> q a n", a=PASSES), rows[r])
 
-        load_x(0, 0, T)
-        load_x(0, 1, T)
         wg_raw = keep.tile([P, PASSES, N], I32, name="wg_raw")
         nc.sync.dma_start(wg_raw[:], wg_words.rearrange("a p n r -> p a (n r)").bitcast(I32))
+        load_x(0, 0)
         wa_raw = keep.tile([P, PASSES * N // 2], I32, name="wa_raw")
         nc.sync.dma_start(
             wa_raw[:].rearrange("p (a n) -> p a n", a=PASSES),
             wa_words.rearrange("a p b -> p a b").bitcast(I32),
         )
-        load_scales(wa_scales, 0)
-        load_x(1, 0, HALF)
         load_scales(wg_scales, WG_ROW)
-        load_x(1, 1, HALF)
+        load_scales(wa_scales, 0)
+        nc.sync.dma_start(offsets[:], offs)
+        load_x(0, 1)
+        load_x(1, 0)
+        load_x(1, 1)
         old_rows = old.rearrange("(p t) c -> t p c", t=PACK)
         page = [keep.tile([P, T], F32, name=f"page{t}") for t in range(PACK)]
         for t in range(PACK):
@@ -79,7 +84,7 @@ def tile_moe_expert_page_fades_where_written_pl_kernel(
         x_scales = [keep.tile([P, J], U8, name=f"x_scales{a}", align_bytes=64) for a in range(PASSES)]
 
         def cast_pairs(engine, pairs, a, u, h, c0, c1):
-            dst = pairs[:, h + c0 : h + c1].bitcast(BF16).rearrange("p (c e) -> p c e", e=2)
+            dst = pairs[:, h * HALF + c0 : h * HALF + c1].bitcast(BF16).rearrange("p (c e) -> p c e", e=2)
             src = x_raw[a, u, h][:, :, c0:c1].rearrange("p e c -> p c e")
             if engine == "vector":
                 nc.vector.tensor_copy(dst, src)
@@ -88,16 +93,12 @@ def tile_moe_expert_page_fades_where_written_pl_kernel(
 
         def gather_x(a, u):
             pairs = keep.tile([P, T], U32, name=f"pairs{a}{u}")
-            if a == 0:
-                cast_pairs("scalar", pairs, a, u, 0, 0, HALF)
-                cast_pairs("vector", pairs, a, u, 0, HALF, T)
-            elif u == 0:
-                cast_pairs("scalar", pairs, a, u, 0, 0, HALF)
-                cast_pairs("scalar", pairs, a, u, HALF, 0, HALF)
+            cast_pairs("scalar", pairs, a, u, 0, 0, HALF)
+            if (a, u) in ((0, 0), (PASSES - 1, 1)):
+                cast_pairs("scalar", pairs, a, u, 1, 0, 192)
+                cast_pairs("vector", pairs, a, u, 1, 192, HALF)
             else:
-                cast_pairs("scalar", pairs, a, u, 0, 0, HALF)
-                cast_pairs("scalar", pairs, a, u, HALF, 0, 192)
-                cast_pairs("vector", pairs, a, u, HALF, 192, HALF)
+                cast_pairs("scalar", pairs, a, u, 1, 0, HALF)
             dst = x_in[a][:].rearrange("p (j u) -> p j u", u=2)[:, :, u]
             nc.vector.tensor_copy(dst, pairs[:].indirect(offsets[:]))
 
@@ -105,10 +106,6 @@ def tile_moe_expert_page_fades_where_written_pl_kernel(
             nc.vector.quantize_mx(
                 out=x_codes[a][:].bitcast(FP8X4), scales=x_scales[a][:], in_=x_in[a][:].bitcast(BF16)
             )
-
-        gather_x(0, 0)
-        gather_x(0, 1)
-        quantize_x(0)
 
         wg = keep.tile([P, PASSES * N], I32, name="wg", align_bytes=64)
         nc.vector.tensor_copy(
@@ -120,18 +117,24 @@ def tile_moe_expert_page_fades_where_written_pl_kernel(
             wa[:].bitcast(U16).rearrange("p (a t m) -> p a m t", a=PASSES, t=PACK),
             wa_raw[:].bitcast(U16).rearrange("p (a m t) -> p a m t", a=PASSES, t=PACK),
         )
+        for q0 in range(0, P, 32):
+            nc.vector.tensor_copy(scale_raw[q0 : q0 + 8, :].bitcast(I32), scale_in[q0 : q0 + 8, :])
         w_scales = keep.tile([P, PASSES * N], U8, name="w_scales", align_bytes=64)
         nc.vector.tensor_copy(
             w_scales[:].rearrange("p (a t m) -> p a m t", a=PASSES, t=PACK),
             scale_raw[:].rearrange("p (a m t) -> p a m t", a=PASSES, t=PACK),
         )
 
+        gather_x(0, 0)
+        gather_x(0, 1)
+        quantize_x(0)
+
         gather_x(1, 0)
         gather_x(1, 1)
         quantize_x(1)
 
-        g_sum = [psum.tile([P, J], F32, name=f"g_sum{t}") for t in range(PACK)]
-        a_sum = [psum.tile([P, J], F32, name=f"a_sum{t}") for t in range(PACK)]
+        g_sum = [psum.tile([P, J], F32, name=f"g_sum{t}", tag=f"bank{2 * t}") for t in range(PACK)]
+        a_sum = [psum.tile([P, J], F32, name=f"a_sum{t}", tag=f"bank{2 * t + 1}") for t in range(PACK)]
         for a in range(PASSES):
             for t in range(PACK):
                 c0 = a * N + t * P
@@ -164,19 +167,56 @@ def tile_moe_expert_page_fades_where_written_pl_kernel(
         picked = keep.tile([P, J], F32, name="picked")
         nc.vector.tensor_copy(picked[:], page[0][:].indirect(offsets[:]))
 
-        lost, minus_a = [], []
+        last = PACK - 1
+        fade, answer = [], []
         for t in range(PACK):
-            fade = keep.tile([P, J], F32, name=f"fade{t}")
-            nc.scalar.activation(fade[:], g_sum[t][:], ACT.Sigmoid, scale=-1.0)
-            neg = keep.tile([P, J], F32, name=f"minus_a{t}")
-            nc.scalar.activation(neg[:], a_sum[t][:], ACT.Copy, scale=-1.0)
-            minus_a.append(neg)
-            prod = keep.tile([P, J], F32, name=f"lost{t}")
-            if t == 0:
-                nc.vector.tensor_tensor(prod[:], picked[:], fade[:], ALU.mult)
+            gone = keep.tile([P, J], F32, name=f"gone{t}")
+            nc.scalar.activation(gone[:], g_sum[t][:], ACT.Sigmoid, scale=-1.0)
+            if t in (0, last):
+                fade.append(gone)
             else:
-                nc.vector.tensor_tensor(prod[:], page[t][:].indirect(offsets[:]), fade[:], ALU.mult)
-            lost.append(prod)
+                minus = keep.tile([P, J], F32, name=f"fade{t}")
+                nc.scalar.activation(minus[:], gone[:], ACT.Copy, scale=-1.0)
+                fade.append(minus)
+            ans = keep.tile([P, J], F32, name=f"answer{t}")
+            nc.scalar.activation(ans[:], a_sum[t][:], ACT.Copy, scale=-1.0 if t == last else 1.0)
+            answer.append(ans)
+
+        def fade_old(t):
+            prod = keep.tile([P, J], F32, name=f"lost{t}", tag=f"lost{min(t, 2)}")
+            if t == 0:
+                nc.vector.scalar_tensor_tensor(prod[:], picked[:], -1.0, fade[t][:], ALU.mult, ALU.mult)
+            else:
+                nc.vector.tensor_tensor(prod[:], page[t][:].indirect(offsets[:]), fade[t][:], ALU.mult)
+            return prod
+
+        def scatter(t, prod):
+            nc.vector.tensor_tensor(faded[t][:].indirect(offsets[:]), prod[:], answer[t][:], ALU.add)
+
+        def turn_and_add(t, c0, bank):
+            turned = psum.tile([P, HALF], F32, name=f"turned{t}{c0}", tag=f"bank{bank}")
+            for b in range(0, HALF, P):
+                cols = slice(c0 + b, c0 + b + P)
+                nc.tensor.matmul(turned[:, b : b + P], page[t][:, cols], identity[:], start=True, stop=False, is_transpose=True)
+                nc.tensor.matmul(turned[:, b : b + P], faded[t][:, cols], identity[:], start=False, stop=True, is_transpose=True)
+            held = keep.tile([P, HALF], F32, name=f"held{t}{c0}")
+            nc.scalar.copy(held[:], turned[:])
+            return held
+
+        def turn_back(t, c0, held, bank):
+            back = psum.tile([P, HALF], F32, name=f"back{t}{c0}", tag=f"bank{bank}")
+            for b in range(0, HALF, P):
+                nc.tensor.transpose(back[:, b : b + P], held[:, b : b + P], identity[:])
+            nc.scalar.copy(y[t // 2][:, t % 2, c0 : c0 + HALF], back[:])
+
+        def add_on_tensor(t, bank, back_bank):
+            held = [turn_and_add(t, h * HALF, bank + h) for h in range(2)]
+            for h in range(2):
+                turn_back(t, h * HALF, held[h], back_bank + h)
+            nc.sync.dma_start(out_rows[t], y[t // 2][:, t % 2, :])
+
+        def add_on_vector(t, c0, c1):
+            nc.vector.tensor_tensor(y[t // 2][:, t % 2, c0:c1], page[t][:, c0:c1], faded[t][:, c0:c1], ALU.subtract if t == last else ALU.add)
 
         def round_pair(engine, u, c0, c1):
             dst = y_in[:].rearrange("p (c r) -> p c r", r=PACK)[:, c0:c1, 2 * u : 2 * u + 2]
@@ -186,23 +226,29 @@ def tile_moe_expert_page_fades_where_written_pl_kernel(
             else:
                 nc.scalar.copy(dst, src)
 
-        for t in range(PACK):
-            nc.vector.tensor_tensor(faded[t][:].indirect(offsets[:]), lost[t][:], minus_a[t][:], ALU.add)
-            if t < PACK - 1:
-                nc.vector.tensor_tensor(y[t // 2][:, t % 2, :], page[t][:], faded[t][:], ALU.subtract)
-                nc.sync.dma_start(out_rows[t], y[t // 2][:, t % 2, :])
-            if t == 1:
-                round_pair("scalar", 0, 0, T)
+        lost = [fade_old(t) for t in range(2)]
+        scatter(0, lost[0])
+        lost.append(fade_old(2))
+        add_on_tensor(0, 0, 2)
+        scatter(1, lost[1])
+        add_on_tensor(1, 2, 0)
+        scatter(2, lost[2])
+        lost.append(fade_old(3))
+        add_on_vector(2, HALF, T)
+        round_pair("scalar", 0, 0, HALF)
+        held = turn_and_add(2, 0, 0)
+        round_pair("scalar", 0, HALF, T)
+        turn_back(2, 0, held, 2)
+        nc.scalar.dma_start(out_rows[2], y[1][:, 0, :])
+        scatter(3, lost[3])
 
-        last = PACK - 1
         for c0 in range(0, T, TAIL):
-            cols = slice(c0, c0 + TAIL)
-            nc.vector.tensor_tensor(y[1][:, 1, cols], page[last][:, cols], faded[last][:, cols], ALU.subtract)
+            add_on_vector(last, c0, c0 + TAIL)
         for c0 in range(0, T, HALF):
             nc.sync.dma_start(out_rows[last][:, c0 : c0 + HALF], y[1][:, 1, c0 : c0 + HALF])
         for c0 in range(0, T, TAIL):
-            round_pair("vector" if c0 >= HALF else "scalar", 1, c0, c0 + TAIL)
-        for c0 in (HALF, 0, HALF + TAIL, TAIL):
+            round_pair("vector" if c0 == T - TAIL else "scalar", 1, c0, c0 + TAIL)
+        for c0 in (0, T - TAIL, TAIL, HALF):
             cols = slice(c0, c0 + TAIL)
             nc.vector.quantize_mx(
                 out=y_codes[:, cols].bitcast(FP8X4),

@@ -48,38 +48,41 @@ def tile_moe_expert_page_fades_where_written_pl_kernel(
         x_rows = xt.rearrange("(a p u e) c -> a u p e c", a=PASSES, p=P, u=2, e=2)
         x_raw = {}
 
-        def load_x(a, u):
-            for h in range(2):
-                raw = keep.tile([P, 2, HALF], F32, name=f"x_raw{a}{u}{h}")
-                nc.sync.dma_start(raw[:], x_rows[a, u, :, :, h * HALF : (h + 1) * HALF])
-                x_raw[a, u, h] = raw
+        def load_x(a, u, h):
+            raw = keep.tile([P, 2, HALF], F32, name=f"x_raw{a}{u}{h}")
+            nc.sync.dma_start(raw[:], x_rows[a, u, :, :, h * HALF : (h + 1) * HALF])
+            x_raw[a, u, h] = raw
 
         def load_scales(scales, row0):
             rows = scales.bitcast(I32).rearrange("a (q r) n -> r q a n", r=4)
             for r in range(4):
                 dst = scale_in[row0 + r : P : 32, :]
-                nc.scalar.dma_start(dst.rearrange("q (a n) -> q a n", a=PASSES), rows[r])
+                nc.sync.dma_start(dst.rearrange("q (a n) -> q a n", a=PASSES), rows[r])
 
+        load_x(0, 0, 0)
+        load_scales(wg_scales, WG_ROW)
+        load_x(0, 0, 1)
+        load_x(0, 1, 0)
+        nc.sync.dma_start(offsets[:], offs)
+        load_scales(wa_scales, 0)
+        load_x(0, 1, 1)
+        for u in range(2):
+            for h in range(2):
+                load_x(1, u, h)
         wg_raw = keep.tile([P, PASSES, N], I32, name="wg_raw")
         nc.sync.dma_start(wg_raw[:], wg_words.rearrange("a p n r -> p a (n r)").bitcast(I32))
-        load_x(0, 0)
         wa_raw = keep.tile([P, PASSES * N // 2], I32, name="wa_raw")
         nc.sync.dma_start(
             wa_raw[:].rearrange("p (a n) -> p a n", a=PASSES),
             wa_words.rearrange("a p b -> p a b").bitcast(I32),
         )
-        load_scales(wg_scales, WG_ROW)
-        load_scales(wa_scales, 0)
-        nc.sync.dma_start(offsets[:], offs)
-        load_x(0, 1)
-        load_x(1, 0)
-        load_x(1, 1)
         old_rows = old.rearrange("(p t) c -> t p c", t=PACK)
         page = [keep.tile([P, T], F32, name=f"page{t}") for t in range(PACK)]
         for t in range(PACK):
             nc.sync.dma_start(page[t][:], old_rows[t])
 
-        x_in = [keep.tile([P, 2 * J], U32, name=f"x_in{a}", align_bytes=64) for a in range(PASSES)]
+        x_in = [keep.tile([P, 2 * J], F32, name=f"x_in{a}", align_bytes=64) for a in range(PASSES)]
+        x_picked = [keep.tile([P, 2 * J], F32, name=f"x_picked{a}") for a in range(PASSES)]
         x_codes = [keep.tile([P, J], U32, name=f"x_codes{a}", align_bytes=64) for a in range(PASSES)]
         x_scales = [keep.tile([P, J], U8, name=f"x_scales{a}", align_bytes=64) for a in range(PASSES)]
 
@@ -89,54 +92,61 @@ def tile_moe_expert_page_fades_where_written_pl_kernel(
             if engine == "vector":
                 nc.vector.tensor_copy(dst, src)
             else:
-                nc.scalar.activation(dst, src, ACT.Copy)
+                nc.scalar.copy(dst, src)
 
         def gather_x(a, u):
-            pairs = keep.tile([P, T], U32, name=f"pairs{a}{u}")
+            pairs = keep.tile([P, T], F32, name=f"pairs{a}{u}")
             cast_pairs("scalar", pairs, a, u, 0, 0, HALF)
             if (a, u) in ((0, 0), (PASSES - 1, 1)):
                 cast_pairs("scalar", pairs, a, u, 1, 0, 192)
                 cast_pairs("vector", pairs, a, u, 1, 192, HALF)
             else:
                 cast_pairs("scalar", pairs, a, u, 1, 0, HALF)
-            dst = x_in[a][:].rearrange("p (j u) -> p j u", u=2)[:, :, u]
-            nc.vector.tensor_copy(dst, pairs[:].indirect(offsets[:]))
+            nc.vector.tensor_copy(x_picked[a][:, u * J : (u + 1) * J], pairs[:].indirect(offsets[:]))
+
+        def weave_x(a):
+            nc.vector.tensor_copy(
+                x_in[a][:].rearrange("p (j u) -> p j u", u=2),
+                x_picked[a][:].rearrange("p (u j) -> p j u", u=2),
+            )
 
         def quantize_x(a):
             nc.vector.quantize_mx(
                 out=x_codes[a][:].bitcast(FP8X4), scales=x_scales[a][:], in_=x_in[a][:].bitcast(BF16)
             )
 
-        wg = keep.tile([P, PASSES * N], I32, name="wg", align_bytes=64)
-        nc.vector.tensor_copy(
-            wg[:].rearrange("p (a t m) -> p a m t", a=PASSES, t=PACK),
-            wg_raw[:].rearrange("p a (m t) -> p a m t", t=PACK),
-        )
-        wa = keep.tile([P, PASSES * N * 2], U8, name="wa", align_bytes=64)
-        nc.vector.tensor_copy(
-            wa[:].bitcast(U16).rearrange("p (a t m) -> p a m t", a=PASSES, t=PACK),
-            wa_raw[:].bitcast(U16).rearrange("p (a m t) -> p a m t", a=PASSES, t=PACK),
-        )
+        gather_x(0, 0)
         for q0 in range(0, P, 32):
             nc.vector.tensor_copy(scale_raw[q0 : q0 + 8, :].bitcast(I32), scale_in[q0 : q0 + 8, :])
         w_scales = keep.tile([P, PASSES * N], U8, name="w_scales", align_bytes=64)
         nc.vector.tensor_copy(
-            w_scales[:].rearrange("p (a t m) -> p a m t", a=PASSES, t=PACK),
-            scale_raw[:].rearrange("p (a m t) -> p a m t", a=PASSES, t=PACK),
+            w_scales[:].rearrange("p (a t m i) -> p a m t i", a=PASSES, t=PACK, i=16),
+            scale_raw[:].rearrange("p (a m i t) -> p a m t i", a=PASSES, t=PACK, i=16),
         )
 
-        gather_x(0, 0)
         gather_x(0, 1)
+        weave_x(0)
         quantize_x(0)
 
         gather_x(1, 0)
         gather_x(1, 1)
+        wg = keep.tile([P, PASSES * N], I32, name="wg", align_bytes=64)
+        nc.vector.tensor_copy(
+            wg[:].rearrange("p (a t m i) -> p a m t i", a=PASSES, t=PACK, i=4),
+            wg_raw[:].rearrange("p a (m i t) -> p a m t i", t=PACK, i=4),
+        )
+        weave_x(1)
         quantize_x(1)
+        wa = keep.tile([P, PASSES * N * 2], U8, name="wa", align_bytes=64)
+        nc.vector.tensor_copy(
+            wa[:].bitcast(U16).rearrange("p (a t m i) -> p a m t i", a=PASSES, t=PACK, i=8),
+            wa_raw[:].bitcast(U16).rearrange("p (a m i t) -> p a m t i", a=PASSES, t=PACK, i=8),
+        )
 
         g_sum = [psum.tile([P, J], F32, name=f"g_sum{t}", tag=f"bank{2 * t}") for t in range(PACK)]
         a_sum = [psum.tile([P, J], F32, name=f"a_sum{t}", tag=f"bank{2 * t + 1}") for t in range(PACK)]
-        for a in range(PASSES):
-            for t in range(PACK):
+        for t in range(PACK):
+            for a in range(PASSES):
                 c0 = a * N + t * P
                 nc.tensor.matmul_mx(
                     out=g_sum[t][:],
@@ -147,6 +157,8 @@ def tile_moe_expert_page_fades_where_written_pl_kernel(
                     start=(a == 0),
                     stop=(a == PASSES - 1),
                 )
+            for a in range(PASSES):
+                c0 = a * N + t * P
                 nc.tensor.matmul_mx(
                     out=a_sum[t][:],
                     lhsT=wa[:, 2 * c0 : 2 * (c0 + P)].bitcast(FP4X4),
@@ -158,7 +170,7 @@ def tile_moe_expert_page_fades_where_written_pl_kernel(
                 )
 
         y = [keep.tile([P, 2, T], F32, name=f"y{u}") for u in range(2)]
-        y_in = keep.tile([P, T * PACK], BF16, name="y_in", align_bytes=64)
+        y_in = keep.tile([P, T * 2], F32, name="y_in", align_bytes=64)
         y_codes = keep.tile([P, T], U32, name="y_codes", align_bytes=64)
         y_scales = keep.tile([P, T], U8, name="y_scales", align_bytes=64)
         out_rows = out_0.rearrange("(p t) c -> t p c", t=PACK)
@@ -218,13 +230,29 @@ def tile_moe_expert_page_fades_where_written_pl_kernel(
         def add_on_vector(t, c0, c1):
             nc.vector.tensor_tensor(y[t // 2][:, t % 2, c0:c1], page[t][:, c0:c1], faded[t][:, c0:c1], ALU.subtract if t == last else ALU.add)
 
-        def round_pair(engine, u, c0, c1):
-            dst = y_in[:].rearrange("p (c r) -> p c r", r=PACK)[:, c0:c1, 2 * u : 2 * u + 2]
-            src = y[u][:, :, c0:c1].rearrange("p e c -> p c e")
+        y_pairs = keep.tile([P, 2 * T], F32, name="y_pairs")
+
+        def move(engine, dst, src):
             if engine == "vector":
                 nc.vector.tensor_copy(dst, src)
             else:
                 nc.scalar.copy(dst, src)
+
+        def round_pair(engine, u, c0, c1):
+            dst = y_pairs[:, u * T + c0 : u * T + c1].bitcast(BF16).rearrange("p (c e) -> p c e", e=2)
+            move(engine, dst, y[u][:, :, c0:c1].rearrange("p e c -> p c e"))
+
+        def weave_y(engine, c0, c1):
+            dst = y_in[:, 2 * c0 : 2 * c1].rearrange("p (c u) -> p c u", u=2)
+            move(engine, dst, y_pairs[:].rearrange("p (u c) -> p c u", u=2)[:, c0:c1, :])
+
+        def quantize_y(c0, c1):
+            nc.vector.quantize_mx(
+                out=y_codes[:, c0:c1].bitcast(FP8X4),
+                scales=y_scales[:, c0:c1],
+                in_=y_in[:, 2 * c0 : 2 * c1].bitcast(BF16),
+            )
+            nc.sync.dma_start(out_words[:, c0:c1], y_codes[:, c0:c1].bitcast(I32))
 
         lost = [fade_old(t) for t in range(2)]
         scatter(0, lost[0])
@@ -242,20 +270,19 @@ def tile_moe_expert_page_fades_where_written_pl_kernel(
         nc.scalar.dma_start(out_rows[2], y[1][:, 0, :])
         scatter(3, lost[3])
 
-        for c0 in range(0, T, TAIL):
-            add_on_vector(last, c0, c0 + TAIL)
+        cuts = (0, TAIL, HALF, T)
+        for c0, c1 in zip(cuts, cuts[1:]):
+            add_on_vector(last, c0, c1)
         for c0 in range(0, T, HALF):
             nc.sync.dma_start(out_rows[last][:, c0 : c0 + HALF], y[1][:, 1, c0 : c0 + HALF])
-        for c0 in range(0, T, TAIL):
-            round_pair("vector" if c0 == T - TAIL else "scalar", 1, c0, c0 + TAIL)
-        for c0 in (0, T - TAIL, TAIL, HALF):
-            cols = slice(c0, c0 + TAIL)
-            nc.vector.quantize_mx(
-                out=y_codes[:, cols].bitcast(FP8X4),
-                scales=y_scales[:, cols],
-                in_=y_in[:, PACK * c0 : PACK * (c0 + TAIL)],
-            )
-            nc.sync.dma_start(out_words[:, cols], y_codes[:, cols].bitcast(I32))
+        for c0 in (0, TAIL):
+            round_pair("scalar", 1, c0, c0 + TAIL)
+            weave_y("scalar", c0, c0 + TAIL)
+        round_pair("vector", 1, HALF, T)
+        quantize_y(0, TAIL)
+        weave_y("vector", HALF, T)
+        quantize_y(TAIL, HALF)
+        quantize_y(HALF, T)
         scale_rows = out_2[0].bitcast(I32).rearrange("(q r) c -> r q c", r=4)
         for r in range(4):
             queue = nc.scalar if r % 2 else nc.sync

from contextlib import ExitStack

import concourse.mybir as mybir
from concourse.masks import make_identity

K, T, J, N = 1024, 1024, 512, 512
FLOPS = 2 * 2 * K * N * J

F32 = mybir.dt.float32
BF16 = mybir.dt.bfloat16
I32 = mybir.dt.int32
U32 = mybir.dt.uint32
U16 = mybir.dt.uint16
U8 = mybir.dt.uint8
FP8X4 = mybir.dt.float8_e4m3fn_x4
FP4X4 = mybir.dt.float4_e2m1fn_x4
ACT = mybir.ActivationFunctionType
ALU = mybir.AluOpType

P = 128
PACK = 4
PASSES = K // (P * PACK)
HALF = T // 2
WG_ROW = 4
TAIL = 256


def tile_moe_expert_page_fades_where_written_pl_kernel(
    tc, xt, wa_words, wa_scales, wg_words, wg_scales, old, offs, out_0, out_1, out_2
):
    nc = tc.nc
    with ExitStack() as ctx:
        keep = ctx.enter_context(tc.tile_pool(name="keep", bufs=1))
        psum = ctx.enter_context(tc.psum_pool(name="psum", bufs=1))

        offsets = keep.tile([P, J // 16], U16, name="offsets")

        scale_raw = keep.tile([P, PASSES * N], U8, name="scale_raw")
        scale_in = keep.tile([P, PASSES * N // 4], I32, name="scale_in")
        nc.vector.memset(scale_raw[:].bitcast(I32), 0)
        faded = [keep.tile([P, T], F32, name=f"faded{t}") for t in range(PACK)]
        for t in range(PACK):
            nc.vector.memset(faded[t][:], 0.0)

        identity = keep.tile([P, P], F32, name="identity")
        make_identity(nc, identity[:])

        x_rows = xt.rearrange("(a p u e) c -> a u p e c", a=PASSES, p=P, u=2, e=2)
        x_raw = {}

        def load_x(a, u, h):
            raw = keep.tile([P, 2, HALF], F32, name=f"x_raw{a}{u}{h}")
            nc.sync.dma_start(raw[:], x_rows[a, u, :, :, h * HALF : (h + 1) * HALF])
            x_raw[a, u, h] = raw

        def load_scales(scales, row0):
            rows = scales.bitcast(I32).rearrange("a (q r) n -> r q a n", r=4)
            for r in range(4):
                dst = scale_in[row0 + r : P : 32, :]
                nc.sync.dma_start(dst.rearrange("q (a n) -> q a n", a=PASSES), rows[r])

        load_x(0, 0, 0)
        load_scales(wg_scales, WG_ROW)
        load_x(0, 0, 1)
        load_x(0, 1, 0)
        nc.sync.dma_start(offsets[:], offs)
        load_scales(wa_scales, 0)
        load_x(0, 1, 1)
        for u in range(2):
            for h in range(2):
                load_x(1, u, h)
        wg_raw = keep.tile([P, PASSES, N], I32, name="wg_raw")
        nc.sync.dma_start(wg_raw[:], wg_words.rearrange("a p n r -> p a (n r)").bitcast(I32))
        wa_raw = keep.tile([P, PASSES * N // 2], I32, name="wa_raw")
        nc.sync.dma_start(
            wa_raw[:].rearrange("p (a n) -> p a n", a=PASSES),
            wa_words.rearrange("a p b -> p a b").bitcast(I32),
        )
        old_rows = old.rearrange("(p t) c -> t p c", t=PACK)
        page = [keep.tile([P, T], F32, name=f"page{t}") for t in range(PACK)]
        for t in range(PACK):
            nc.sync.dma_start(page[t][:], old_rows[t])

        x_in = [keep.tile([P, 2 * J], F32, name=f"x_in{a}", align_bytes=64) for a in range(PASSES)]
        x_picked = [keep.tile([P, 2 * J], F32, name=f"x_picked{a}") for a in range(PASSES)]
        x_codes = [keep.tile([P, J], U32, name=f"x_codes{a}", align_bytes=64) for a in range(PASSES)]
        x_scales = [keep.tile([P, J], U8, name=f"x_scales{a}", align_bytes=64) for a in range(PASSES)]

        def cast_pairs(engine, pairs, a, u, h, c0, c1):
            dst = pairs[:, h * HALF + c0 : h * HALF + c1].bitcast(BF16).rearrange("p (c e) -> p c e", e=2)
            src = x_raw[a, u, h][:, :, c0:c1].rearrange("p e c -> p c e")
            if engine == "vector":
                nc.vector.tensor_copy(dst, src)
            else:
                nc.scalar.copy(dst, src)

        def gather_x(a, u):
            pairs = keep.tile([P, T], F32, name=f"pairs{a}{u}")
            cast_pairs("scalar", pairs, a, u, 0, 0, HALF)
            if (a, u) in ((0, 0), (PASSES - 1, 1)):
                cast_pairs("scalar", pairs, a, u, 1, 0, 192)
                cast_pairs("vector", pairs, a, u, 1, 192, HALF)
            else:
                cast_pairs("scalar", pairs, a, u, 1, 0, HALF)
            nc.vector.tensor_copy(x_picked[a][:, u * J : (u + 1) * J], pairs[:].indirect(offsets[:]))

        def weave_x(a):
            nc.vector.tensor_copy(
                x_in[a][:].rearrange("p (j u) -> p j u", u=2),
                x_picked[a][:].rearrange("p (u j) -> p j u", u=2),
            )

        def quantize_x(a):
            nc.vector.quantize_mx(
                out=x_codes[a][:].bitcast(FP8X4), scales=x_scales[a][:], in_=x_in[a][:].bitcast(BF16)
            )

        gather_x(0, 0)
        for q0 in range(0, P, 32):
            nc.vector.tensor_copy(scale_raw[q0 : q0 + 8, :].bitcast(I32), scale_in[q0 : q0 + 8, :])
        w_scales = keep.tile([P, PASSES * N], U8, name="w_scales", align_bytes=64)
        nc.vector.tensor_copy(
            w_scales[:].rearrange("p (a t m i) -> p a m t i", a=PASSES, t=PACK, i=16),
            scale_raw[:].rearrange("p (a m i t) -> p a m t i", a=PASSES, t=PACK, i=16),
        )

        gather_x(0, 1)
        weave_x(0)
        quantize_x(0)

        gather_x(1, 0)
        gather_x(1, 1)
        wg = keep.tile([P, PASSES * N], I32, name="wg", align_bytes=64)
        nc.vector.tensor_copy(
            wg[:].rearrange("p (a t m i) -> p a m t i", a=PASSES, t=PACK, i=4),
            wg_raw[:].rearrange("p a (m i t) -> p a m t i", t=PACK, i=4),
        )
        weave_x(1)
        quantize_x(1)
        wa = keep.tile([P, PASSES * N * 2], U8, name="wa", align_bytes=64)
        nc.vector.tensor_copy(
            wa[:].bitcast(U16).rearrange("p (a t m i) -> p a m t i", a=PASSES, t=PACK, i=8),
            wa_raw[:].bitcast(U16).rearrange("p (a m i t) -> p a m t i", a=PASSES, t=PACK, i=8),
        )

        g_sum = [psum.tile([P, J], F32, name=f"g_sum{t}", tag=f"bank{2 * t}") for t in range(PACK)]
        a_sum = [psum.tile([P, J], F32, name=f"a_sum{t}", tag=f"bank{2 * t + 1}") for t in range(PACK)]
        for t in range(PACK):
            for a in range(PASSES):
                c0 = a * N + t * P
                nc.tensor.matmul_mx(
                    out=g_sum[t][:],
                    lhsT=wg[:, c0 : c0 + P].bitcast(FP8X4),
                    lhsT_scale=w_scales[WG_ROW:P, c0 : c0 + P],
                    rhs=x_codes[a][:].bitcast(FP8X4),
                    rhs_scale=x_scales[a][:],
                    start=(a == 0),
                    stop=(a == PASSES - 1),
                )
            for a in range(PASSES):
                c0 = a * N + t * P
                nc.tensor.matmul_mx(
                    out=a_sum[t][:],
                    lhsT=wa[:, 2 * c0 : 2 * (c0 + P)].bitcast(FP4X4),
                    lhsT_scale=w_scales[:, c0 : c0 + P],
                    rhs=x_codes[a][:].bitcast(FP8X4),
                    rhs_scale=x_scales[a][:],
                    start=(a == 0),
                    stop=(a == PASSES - 1),
                )

        y = [keep.tile([P, 2, T], F32, name=f"y{u}") for u in range(2)]
        y_in = keep.tile([P, T * 2], F32, name="y_in", align_bytes=64)
        y_codes = keep.tile([P, T], U32, name="y_codes", align_bytes=64)
        y_scales = keep.tile([P, T], U8, name="y_scales", align_bytes=64)
        out_rows = out_0.rearrange("(p t) c -> t p c", t=PACK)
        out_words = out_1[0].rearrange("p c r -> p (c r)").bitcast(I32)

        picked = keep.tile([P, J], F32, name="picked")
        nc.vector.tensor_copy(picked[:], page[0][:].indirect(offsets[:]))

        last = PACK - 1
        fade, answer = [], []
        for t in range(PACK):
            gone = keep.tile([P, J], F32, name=f"gone{t}")
            nc.scalar.activation(gone[:], g_sum[t][:], ACT.Sigmoid, scale=-1.0)
            if t in (0, last):
                fade.append(gone)
            else:
                minus = keep.tile([P, J], F32, name=f"fade{t}")
                nc.scalar.activation(minus[:], gone[:], ACT.Copy, scale=-1.0)
                fade.append(minus)
            ans = keep.tile([P, J], F32, name=f"answer{t}")
            nc.scalar.activation(ans[:], a_sum[t][:], ACT.Copy, scale=-1.0 if t == last else 1.0)
            answer.append(ans)

        def fade_old(t):
            prod = keep.tile([P, J], F32, name=f"lost{t}", tag=f"lost{min(t, 2)}")
            if t == 0:
                nc.vector.scalar_tensor_tensor(prod[:], picked[:], -1.0, fade[t][:], ALU.mult, ALU.mult)
            else:
                nc.vector.tensor_tensor(prod[:], page[t][:].indirect(offsets[:]), fade[t][:], ALU.mult)
            return prod

        def scatter(t, prod):
            nc.vector.tensor_tensor(faded[t][:].indirect(offsets[:]), prod[:], answer[t][:], ALU.add)

        def turn_and_add(t, c0, bank):
            turned = psum.tile([P, HALF], F32, name=f"turned{t}{c0}", tag=f"bank{bank}")
            for b in range(0, HALF, P):
                cols = slice(c0 + b, c0 + b + P)
                nc.tensor.matmul(turned[:, b : b + P], page[t][:, cols], identity[:], start=True, stop=False, is_transpose=True)
                nc.tensor.matmul(turned[:, b : b + P], faded[t][:, cols], identity[:], start=False, stop=True, is_transpose=True)
            held = keep.tile([P, HALF], F32, name=f"held{t}{c0}")
            nc.scalar.copy(held[:], turned[:])
            return held

        def turn_back(t, c0, held, bank):
            back = psum.tile([P, HALF], F32, name=f"back{t}{c0}", tag=f"bank{bank}")
            for b in range(0, HALF, P):
                nc.tensor.transpose(back[:, b : b + P], held[:, b : b + P], identity[:])
            nc.scalar.copy(y[t // 2][:, t % 2, c0 : c0 + HALF], back[:])

        def add_on_tensor(t, bank, back_bank):
            held = [turn_and_add(t, h * HALF, bank + h) for h in range(2)]
            for h in range(2):
                turn_back(t, h * HALF, held[h], back_bank + h)
            nc.sync.dma_start(out_rows[t], y[t // 2][:, t % 2, :])

        def add_on_vector(t, c0, c1):
            nc.vector.tensor_tensor(y[t // 2][:, t % 2, c0:c1], page[t][:, c0:c1], faded[t][:, c0:c1], ALU.subtract if t == last else ALU.add)

        y_pairs = keep.tile([P, 2 * T], F32, name="y_pairs")

        def move(engine, dst, src):
            if engine == "vector":
                nc.vector.tensor_copy(dst, src)
            else:
                nc.scalar.copy(dst, src)

        def round_pair(engine, u, c0, c1):
            dst = y_pairs[:, u * T + c0 : u * T + c1].bitcast(BF16).rearrange("p (c e) -> p c e", e=2)
            move(engine, dst, y[u][:, :, c0:c1].rearrange("p e c -> p c e"))

        def weave_y(engine, c0, c1):
            dst = y_in[:, 2 * c0 : 2 * c1].rearrange("p (c u) -> p c u", u=2)
            move(engine, dst, y_pairs[:].rearrange("p (u c) -> p c u", u=2)[:, c0:c1, :])

        def quantize_y(c0, c1):
            nc.vector.quantize_mx(
                out=y_codes[:, c0:c1].bitcast(FP8X4),
                scales=y_scales[:, c0:c1],
                in_=y_in[:, 2 * c0 : 2 * c1].bitcast(BF16),
            )
            nc.sync.dma_start(out_words[:, c0:c1], y_codes[:, c0:c1].bitcast(I32))

        lost = [fade_old(t) for t in range(2)]
        scatter(0, lost[0])
        lost.append(fade_old(2))
        add_on_tensor(0, 0, 2)
        scatter(1, lost[1])
        add_on_tensor(1, 2, 0)
        scatter(2, lost[2])
        lost.append(fade_old(3))
        add_on_vector(2, HALF, T)
        round_pair("scalar", 0, 0, HALF)
        held = turn_and_add(2, 0, 0)
        round_pair("scalar", 0, HALF, T)
        turn_back(2, 0, held, 2)
        nc.scalar.dma_start(out_rows[2], y[1][:, 0, :])
        scatter(3, lost[3])

        cuts = (0, TAIL, HALF, T)
        for c0, c1 in zip(cuts, cuts[1:]):
            add_on_vector(last, c0, c1)
        for c0 in range(0, T, HALF):
            nc.sync.dma_start(out_rows[last][:, c0 : c0 + HALF], y[1][:, 1, c0 : c0 + HALF])
        for c0 in (0, TAIL):
            round_pair("scalar", 1, c0, c0 + TAIL)
            weave_y("scalar", c0, c0 + TAIL)
        round_pair("vector", 1, HALF, T)
        quantize_y(0, TAIL)
        weave_y("vector", HALF, T)
        quantize_y(TAIL, HALF)
        quantize_y(HALF, T)
        scale_rows = out_2[0].bitcast(I32).rearrange("(q r) c -> r q c", r=4)
        for r in range(4):
            queue = nc.scalar if r % 2 else nc.sync
            queue.dma_start(scale_rows[r], y_scales[r:P:32, :].bitcast(I32))
